import numpy as np
import ml_dtypes


def mxq(x, axis, fmt="e4m3"):
    dtype, down = {"e4m3": (ml_dtypes.float8_e4m3fn, 7), "e5m2": (ml_dtypes.float8_e5m2, 14)}[fmt]
    v = np.moveaxis(np.asarray(x, np.float32).astype(ml_dtypes.bfloat16).astype(np.float64), axis, -1)
    blocks = v.reshape(v.shape[:-1] + (-1, 32))
    amax = np.abs(blocks).max(-1, keepdims=True)
    byte = np.maximum(np.where(amax > 0, np.frexp(amax)[1] - 1 + 127, 0) - down, 1)
    scale = np.exp2(byte - 127.0)
    codes = (blocks / scale).astype(np.float32).astype(dtype).astype(np.float64)
    return np.moveaxis((codes * scale).reshape(v.shape), -1, axis)


WIDE = False


def mx_kscale(k):
    if not WIDE:
        return np.ones(k)
    levels = np.array([10, -10, 5, -5, 0])
    if k % 512:
        return np.exp2(np.random.permutation(np.resize(levels, k // 32))).repeat(32)
    a = np.empty((k // 512, 16))
    for p in range(k // 512):
        a[p, :8] = np.random.permutation(np.resize(levels, 8))
        for g in range(8):
            far = levels[np.abs(levels - a[p, g]) >= 10]
            a[p, g + 8] = far[np.random.randint(len(far))]
    return np.exp2(a.ravel()).repeat(32)


BF16 = ml_dtypes.bfloat16


def bf(x):
    return np.asarray(x, np.float32).astype(BF16)


def f64(x):
    return np.asarray(x).astype(np.float64)


E2M1 = np.array([0.0, 0.5, 1.0, 1.5, 2.0, 3.0, 4.0, 6.0, -0.0, -0.5, -1.0, -1.5, -2.0, -3.0, -4.0, -6.0])


def pack_weight(w, fmt):
    k, n = w.shape
    w = f64(bf(w)).reshape(k // 32, 32, n)
    amax = np.abs(w).max(1)
    if fmt == "e4m3":
        byte = np.frexp(amax)[1] - 1 + 127 - 7
    else:
        mant, ex = np.frexp(amax / 6.0)
        byte = np.where(mant > 0.5, ex, ex - 1) + 127
    byte = np.clip(np.where(amax > 0, byte, 1), 1, 254)
    scaled = (w * np.exp2(127.0 - byte)[:, None, :]).reshape(k, n).astype(np.float32)
    by_word = np.ascontiguousarray(scaled.reshape(k // 512, 128, 4, n).transpose(0, 1, 3, 2))
    if fmt == "e4m3":
        words = by_word.astype(ml_dtypes.float8_e4m3fn).view(np.uint8)
    else:
        c = by_word.astype(ml_dtypes.float4_e2m1fn).view(np.uint8) & 0xF
        words = c[..., 0::2] | (c[..., 1::2] << 4)
    return np.ascontiguousarray(words), np.ascontiguousarray(byte.astype(np.uint8).reshape(k // 512, 16, n))


def unpack_weight(words, scales, fmt):
    g, p, n, _ = words.shape
    if fmt == "e4m3":
        vals = np.ascontiguousarray(words).view(ml_dtypes.float8_e4m3fn).astype(np.float64)
    else:
        nib = np.empty((g, p, n, 4), np.uint8)
        nib[..., 0::2] = words & 0xF
        nib[..., 1::2] = words >> 4
        vals = E2M1[nib]
    vals = vals * np.repeat(np.exp2(scales.astype(np.float64) - 127.0), 8, axis=1)[..., None]
    return vals.transpose(0, 1, 3, 2).reshape(g * 512, n)
def pack4(w):
    words, scales = pack_weight(w, "e2m1")
    return words.reshape(words.shape[0], 128, -1), scales


def unpack4(words, scales):
    return unpack_weight(words.reshape(words.shape[0], 128, -1, 2), scales, "e2m1")


def planes(Y):
    n, m = Y.shape
    b = f64(bf(Y)).reshape(n // 32, 32, m)
    amax = np.abs(b).max(1)
    byte = np.clip(np.where(amax > 0, np.frexp(amax)[1] - 1 + 127 - 7, 1), 1, 254)
    codes = (b * np.exp2(127.0 - byte)[:, None, :]).reshape(n, m).astype(np.float32).astype(ml_dtypes.float8_e4m3fn).view(np.uint8)
    words = codes.reshape(n // 512, 128, 4, m).transpose(0, 1, 3, 2)
    return np.ascontiguousarray(words), np.ascontiguousarray(byte.astype(np.uint8).reshape(n // 512, 16, m))


S, R, B, D = 2048, 1024, 4, 512

def setup_inputs():
    s = mx_kscale(S)
    v = np.random.randn(S, B * D) / s[:, None]
    v_words, v_scales = pack_weight(f64(bf(v)), "e4m3")
    spread = np.exp(0.8 * np.random.randn(R))
    compress = np.random.randn(S, R) / np.sqrt(S) * spread[None, :] * s[:, None]
    seq_factor = 0.5 + np.random.rand(B)
    slot_bias = 0.4 * np.random.randn(R)
    return {
        "v_words": v_words,
        "v_scales": v_scales,
        "compress": bf(compress),
        "seq_factor": bf(seq_factor),
        "slot_bias": bf(slot_bias),
    }

def reference(v_words, v_scales, compress, seq_factor, slot_bias):
    v = unpack_weight(v_words, v_scales, "e4m3")
    e = mxq(f64(compress), 0, "e4m3")
    c = (e.T @ v).reshape(R, B, D)
    y = c * f64(seq_factor)[None, :, None] + f64(slot_bias)[:, None, None]
    words, scales = planes(y.reshape(R, B * D))
    return y, words, scales

@@ -1,0 +1,260 @@
+from contextlib import ExitStack
+
+import concourse.mybir as mybir
+
+S, R, B, D = 2048, 1024, 4, 512
+FLOPS = 2 * S * R * B * D
+
+F32 = mybir.dt.float32
+BF16 = mybir.dt.bfloat16
+I32 = mybir.dt.int32
+U32 = mybir.dt.uint32
+U8 = mybir.dt.uint8
+FP8X4 = mybir.dt.float8_e4m3fn_x4
+IDENT = mybir.ActivationFunctionType.Identity
+
+P = 128
+PACK = 4
+GROUP = P * PACK
+PASSES = S // GROUP
+HALVES = R // GROUP
+COLS = B * D
+VEC_M = 84
+
+
+def tile_sequence_compressed_values_g6_kernel(
+    tc, v_words, v_scales, compress, seq_factor, slot_bias, out_0, out_1, out_2
+):
+    nc = tc.nc
+    with ExitStack() as ctx:
+        keep = ctx.enter_context(tc.tile_pool(name="keep", bufs=1))
+        stage = ctx.enter_context(tc.tile_pool(name="stage", bufs=3))
+        psum = ctx.enter_context(tc.psum_pool(name="psum", bufs=1))
+        ctx.enter_context(tc.manual_schedule())
+
+        v_plane = keep.tile([P, COLS], U8, align_bytes=256)
+        seed = keep.tile([P, 32], BF16, align_bytes=64)
+        seed_t = keep.tile([P, 32], BF16, align_bytes=64)
+        spread = keep.tile([P, 32], F32, align_bytes=64)
+        factor = keep.tile([P, 32], F32, align_bytes=64)
+        bias = keep.tile([P, HALVES, PACK], BF16, align_bytes=64)
+        warm = keep.tile([P, 1], F32, align_bytes=64)
+        v_codes = {}
+        raw = {}
+        c_codes = {}
+        c_plane = {}
+        for g in range(PASSES):
+            for pair in range(2):
+                v_codes[g, pair] = keep.tile([P, 2 * D], U32, align_bytes=256, name=f"v{g}{pair}")
+            for h in range(HALVES):
+                raw[h, g] = keep.tile([P, PACK, GROUP], BF16, align_bytes=256, name=f"raw{h}{g}")
+                c_codes[h, g] = keep.tile([P, GROUP], U32, align_bytes=256, name=f"cc{h}{g}")
+                c_plane[h, g] = keep.tile([P, GROUP], U8, align_bytes=256, name=f"cs{h}{g}")
+        y = {}
+        y_codes = {}
+        y_plane = {}
+        for h in range(HALVES):
+            y[h] = keep.tile([P, PACK, COLS], F32, align_bytes=256, name=f"y{h}")
+            y_codes[h] = keep.tile([P, COLS], U32, align_bytes=256, name=f"yc{h}")
+            y_plane[h] = keep.tile([P, COLS], U8, align_bytes=256, name=f"ys{h}")
+
+        def load_c(h, g):
+            rows = compress[g * GROUP : (g + 1) * GROUP, h * GROUP : (h + 1) * GROUP]
+            nc.sync.dma_start(out=raw[h, g][:], in_=rows.rearrange("(p j) c -> p j c", j=PACK))
+
+        def load_v(g, pair):
+            flat = v_words[g].rearrange("p n t -> p (n t)")
+            width = 2 * D * PACK
+            nc.sync.dma_start(
+                out=v_codes[g, pair][:].bitcast(I32),
+                in_=flat[:, pair * width : (pair + 1) * width].bitcast(I32),
+            )
+
+        def load_scales(eng, q):
+            eng.dma_start(
+                out=v_plane[32 * q : 32 * q + 16, :].bitcast(I32),
+                in_=v_scales[:, 4 * q : 4 * q + 4, :].bitcast(I32),
+            )
+
+        c_grouped = {}
+
+        def group_c(h, g, split):
+            tile = stage.tile([P, PACK * GROUP], BF16, align_bytes=256, name="c_grouped")
+            c_grouped[h, g] = tile
+            dst = tile[:].rearrange("p (t m j) -> p m t j", t=PACK, j=PACK)
+            src = raw[h, g][:].rearrange("p j (m t) -> p m t j", t=PACK)
+            if split:
+                nc.vector.tensor_copy(out=dst[:, :VEC_M], in_=src[:, :VEC_M])
+                nc.scalar.copy(out=dst[:, VEC_M:], in_=src[:, VEC_M:])
+            else:
+                nc.vector.tensor_copy(out=dst, in_=src)
+
+        def quant_c(h, g, parts):
+            w = GROUP // parts
+            for i in range(parts):
+                nc.vector.quantize_mx(
+                    out=c_codes[h, g][:, i * w : (i + 1) * w].bitcast(FP8X4),
+                    scales=c_plane[h, g][:, i * w : (i + 1) * w],
+                    in_=c_grouped[h, g][:, PACK * i * w : PACK * (i + 1) * w],
+                )
+
+        acc = {}
+
+        def mm(h, t, c0, w, g, bank):
+            if g == 0:
+                acc[h, t, c0] = psum.tile([P, w], F32, name=f"bank{bank}")
+            pair, off = divmod(c0, 2 * D)
+            nc.tensor.matmul_mx(
+                out=acc[h, t, c0][:],
+                lhsT=c_codes[h, g][:, t * P : (t + 1) * P].bitcast(FP8X4),
+                lhsT_scale=c_plane[h, g][:, t * P : (t + 1) * P],
+                rhs=v_codes[g, pair][:, off : off + w].bitcast(FP8X4),
+                rhs_scale=v_plane[PACK * g :, c0 : c0 + w],
+                start=(g == 0),
+                stop=(g == PASSES - 1),
+            )
+
+        def drain(h, t, c0, w):
+            b = c0 // D
+            nc.scalar.activation(
+                out=y[h][:, t, c0 : c0 + w],
+                in_=acc[h, t, c0][:],
+                func=IDENT,
+                bias=bias[:, h, t : t + 1],
+                scale=factor[:, b : b + 1],
+            )
+
+        y_grouped = {}
+
+        def group_y(h, c0, w):
+            tile = stage.tile([P, PACK * w], BF16, align_bytes=256, name="y_grouped")
+            y_grouped[h, c0] = tile
+            nc.vector.tensor_copy(
+                out=tile[:].rearrange("p (c i t) -> p c t i", i=4, t=PACK),
+                in_=y[h][:, :, c0 : c0 + w].rearrange("p t (c i) -> p c t i", i=4),
+            )
+
+        def quant_y(h, c0, w):
+            nc.vector.quantize_mx(
+                out=y_codes[h][:, c0 : c0 + w].bitcast(FP8X4),
+                scales=y_plane[h][:, c0 : c0 + w],
+                in_=y_grouped[h, c0][:],
+            )
+
+        def store_y(h, t0, t1, c0, c1):
+            rows = out_0[h * GROUP : (h + 1) * GROUP].rearrange("(p t) b d -> p t (b d)", t=PACK)
+            nc.sync.dma_start(out=rows[:, t0:t1, c0:c1], in_=y[h][:, t0:t1, c0:c1])
+
+        def store_codes(h, c0, c1):
+            flat = out_1[h].rearrange("p n t -> p (n t)")
+            nc.sync.dma_start(
+                out=flat[:, PACK * c0 : PACK * c1].bitcast(I32),
+                in_=y_codes[h][:, c0:c1].bitcast(I32),
+            )
+
+        def store_scales(eng, h, q):
+            eng.dma_start(
+                out=out_2[h, 4 * q : 4 * q + 4, :].bitcast(I32),
+                in_=y_plane[h][32 * q : 32 * q + 4, :].bitcast(I32),
+            )
+
+        nc.vector.memset(v_plane[:].bitcast(I32), 0)
+        nc.vector.memset(seed[:], 0.0)
+        load_c(0, 0)
+        load_scales(nc.scalar, 0)
+        load_scales(nc.scalar, 1)
+        load_scales(nc.gpsimd, 2)
+        load_scales(nc.gpsimd, 3)
+        nc.scalar.activation(out=warm[:], in_=seed[:, 16:17], func=IDENT)
+        load_v(0, 0)
+        nc.sync.dma_start(out=seed[0:P:32, 0:B], in_=seq_factor.partition_broadcast(4))
+        for g in range(1, PASSES):
+            load_c(0, g)
+            load_v(g, 0)
+        nc.sync.dma_start(out=bias[:], in_=slot_bias.rearrange("(h p t) -> p h t", h=HALVES, t=PACK))
+        for g in range(PASSES):
+            load_v(g, 1)
+        for g in range(PASSES):
+            load_c(1, g)
+
+        for g in range(PASSES):
+            group_c(0, g, True)
+            if g == 1:
+                nc.vector.transpose(out=seed_t[:], in_=seed[:])
+            if g == 2:
+                nc.vector.tensor_copy(out=spread[:], in_=seed_t[:, 0:1].to_broadcast([P, 32]))
+            if g == 3:
+                nc.vector.transpose(out=factor[:], in_=spread[:])
+            quant_c(0, g, 2)
+            if g < PASSES - 1:
+                order = [(b, t) for t in range(PACK) for b in range(2)]
+            else:
+                order = [(b, t) for b in range(2) for t in range(PACK)]
+            for b, t in order:
+                mm(0, t, b * D, D, g, 4 * b + t)
+        for b in range(2):
+            for t in range(PACK):
+                drain(0, t, b * D, D)
+        for t in (0, 2):
+            store_y(0, t, t + 2, 0, 2 * D)
+        group_y(0, 0, D)
+        quant_y(0, 0, D)
+
+        group_c(1, 0, False)
+        for g in range(1, PASSES):
+            group_c(1, g, False)
+            quant_c(1, g - 1, 1)
+        quant_c(1, PASSES - 1, 1)
+
+        def unit(h, c0, w, bank0, pass_major):
+            if pass_major:
+                for g in range(PASSES):
+                    for t in range(PACK):
+                        mm(h, t, c0, w, g, bank0 + t)
+                for t in range(PACK):
+                    drain(h, t, c0, w)
+            else:
+                for t in range(PACK):
+                    for g in range(PASSES):
+                        mm(h, t, c0, w, g, bank0 + t)
+                    drain(h, t, c0, w)
+
+        unit(0, 2 * D, D, 0, True)
+        unit(0, 3 * D, D, 4, False)
+        for t in (0, 2):
+            store_y(0, t, t + 2, 2 * D, COLS)
+        group_y(0, D, D)
+        group_y(0, 2 * D, D)
+        quant_y(0, D, D)
+        group_y(0, 3 * D, D)
+        quant_y(0, 2 * D, D)
+        unit(1, 0, D, 0, True)
+        group_y(1, 0, D)
+        quant_y(0, 3 * D, D)
+        quant_y(1, 0, D)
+        unit(1, D, D, 4, False)
+        store_y(1, 0, 2, 0, 2 * D)
+        store_codes(0, 0, COLS)
+        for q in range(4):
+            store_scales(nc.sync, 0, q)
+        store_y(1, 2, 4, 0, 2 * D)
+        group_y(1, D, D)
+        quant_y(1, D, D)
+        store_codes(1, 0, 2 * D)
+        unit(1, 2 * D, D, 0, False)
+        store_y(1, 0, 4, 2 * D, 3 * D)
+        group_y(1, 2 * D, D)
+        quant_y(1, 2 * D, D)
+        half = D // 2
+        unit(1, 3 * D, half, 4, False)
+        store_y(1, 0, 4, 3 * D, 3 * D + half)
+        group_y(1, 3 * D, half)
+        quant_y(1, 3 * D, half)
+        store_codes(1, 2 * D, 3 * D + half)
+        unit(1, 3 * D + half, half, 0, False)
+        store_y(1, 0, 4, 3 * D + half, COLS)
+        group_y(1, 3 * D + half, half)
+        quant_y(1, 3 * D + half, half)
+        store_codes(1, 3 * D + half, COLS)
+        for q in range(4):
+            store_scales(nc.scalar if q % 2 else nc.sync, 1, q)

@@ -19,7 +19,6 @@ GROUP = P * PACK
 PASSES = S // GROUP
 HALVES = R // GROUP
 COLS = B * D
-VEC_M = 84
 
 
 def tile_sequence_compressed_values_g6_kernel(
@@ -28,7 +27,7 @@ def tile_sequence_compressed_values_g6_kernel(
     nc = tc.nc
     with ExitStack() as ctx:
         keep = ctx.enter_context(tc.tile_pool(name="keep", bufs=1))
-        stage = ctx.enter_context(tc.tile_pool(name="stage", bufs=3))
+        stage = ctx.enter_context(tc.tile_pool(name="stage", bufs=4))
         psum = ctx.enter_context(tc.psum_pool(name="psum", bufs=1))
         ctx.enter_context(tc.manual_schedule())
 
@@ -54,21 +53,32 @@ def tile_sequence_compressed_values_g6_kernel(
         y_codes = {}
         y_plane = {}
         for h in range(HALVES):
-            y[h] = keep.tile([P, PACK, COLS], F32, align_bytes=256, name=f"y{h}")
             y_codes[h] = keep.tile([P, COLS], U32, align_bytes=256, name=f"yc{h}")
             y_plane[h] = keep.tile([P, COLS], U8, align_bytes=256, name=f"ys{h}")
+
+        y_spans = [(0, 0, 2 * D), (0, 2 * D, COLS), (1, 0, 2 * D), (1, 2 * D, 3 * D), (1, 3 * D, 3 * D + D // 2), (1, 3 * D + D // 2, COLS)]
+        for h, c0, c1 in y_spans:
+            y[h, c0, c1] = keep.tile([P, PACK, c1 - c0], F32, align_bytes=256, name=f"y{h}_{c0}")
+
+        def y_view(h, t0, t1, c0, c1):
+            for hh, a, b in y_spans:
+                if hh == h and a <= c0 and c1 <= b:
+                    return y[hh, a, b][:, t0:t1, c0 - a : c1 - a]
+            raise ValueError("no such span")
 
         def load_c(h, g):
             rows = compress[g * GROUP : (g + 1) * GROUP, h * GROUP : (h + 1) * GROUP]
             nc.sync.dma_start(out=raw[h, g][:], in_=rows.rearrange("(p j) c -> p j c", j=PACK))
 
-        def load_v(g, pair):
+        def load_v(g, pair, parts=1):
             flat = v_words[g].rearrange("p n t -> p (n t)")
-            width = 2 * D * PACK
-            nc.sync.dma_start(
-                out=v_codes[g, pair][:].bitcast(I32),
-                in_=flat[:, pair * width : (pair + 1) * width].bitcast(I32),
-            )
+            w = 2 * D // parts
+            for i in range(parts):
+                c0 = pair * 2 * D + i * w
+                nc.sync.dma_start(
+                    out=v_codes[g, pair][:, i * w : (i + 1) * w].bitcast(I32),
+                    in_=flat[:, PACK * c0 : PACK * (c0 + w)].bitcast(I32),
+                )
 
         def load_scales(eng, q):
             eng.dma_start(
@@ -78,25 +88,19 @@ def tile_sequence_compressed_values_g6_kernel(
 
         c_grouped = {}
 
-        def group_c(h, g, split):
-            tile = stage.tile([P, PACK * GROUP], BF16, align_bytes=256, name="c_grouped")
-            c_grouped[h, g] = tile
-            dst = tile[:].rearrange("p (t m j) -> p m t j", t=PACK, j=PACK)
+        def group_c(copy, h, g, t0, t1):
+            if t0 == 0:
+                c_grouped[h, g] = stage.tile([P, PACK * GROUP], BF16, align_bytes=256, name="c_grouped")
+            dst = c_grouped[h, g][:].rearrange("p (t m j) -> p m t j", t=PACK, j=PACK)
             src = raw[h, g][:].rearrange("p j (m t) -> p m t j", t=PACK)
-            if split:
-                nc.vector.tensor_copy(out=dst[:, :VEC_M], in_=src[:, :VEC_M])
-                nc.scalar.copy(out=dst[:, VEC_M:], in_=src[:, VEC_M:])
-            else:
-                nc.vector.tensor_copy(out=dst, in_=src)
+            copy(out=dst[:, :, t0:t1], in_=src[:, :, t0:t1])
 
-        def quant_c(h, g, parts):
-            w = GROUP // parts
-            for i in range(parts):
-                nc.vector.quantize_mx(
-                    out=c_codes[h, g][:, i * w : (i + 1) * w].bitcast(FP8X4),
-                    scales=c_plane[h, g][:, i * w : (i + 1) * w],
-                    in_=c_grouped[h, g][:, PACK * i * w : PACK * (i + 1) * w],
-                )
+        def quant_c(h, g, t0, t1):
+            nc.vector.quantize_mx(
+                out=c_codes[h, g][:, t0 * P : t1 * P].bitcast(FP8X4),
+                scales=c_plane[h, g][:, t0 * P : t1 * P],
+                in_=c_grouped[h, g][:, t0 * GROUP : t1 * GROUP],
+            )
 
         acc = {}
 
@@ -117,7 +121,7 @@ def tile_sequence_compressed_values_g6_kernel(
         def drain(h, t, c0, w):
             b = c0 // D
             nc.scalar.activation(
-                out=y[h][:, t, c0 : c0 + w],
+                out=y_view(h, t, t + 1, c0, c0 + w)[:, 0],
                 in_=acc[h, t, c0][:],
                 func=IDENT,
                 bias=bias[:, h, t : t + 1],
@@ -131,7 +135,7 @@ def tile_sequence_compressed_values_g6_kernel(
             y_grouped[h, c0] = tile
             nc.vector.tensor_copy(
                 out=tile[:].rearrange("p (c i t) -> p c t i", i=4, t=PACK),
-                in_=y[h][:, :, c0 : c0 + w].rearrange("p t (c i) -> p c t i", i=4),
+                in_=y_view(h, 0, PACK, c0, c0 + w).rearrange("p t (c i) -> p c t i", i=4),
             )
 
         def quant_y(h, c0, w):
@@ -143,7 +147,7 @@ def tile_sequence_compressed_values_g6_kernel(
 
         def store_y(h, t0, t1, c0, c1):
             rows = out_0[h * GROUP : (h + 1) * GROUP].rearrange("(p t) b d -> p t (b d)", t=PACK)
-            nc.sync.dma_start(out=rows[:, t0:t1, c0:c1], in_=y[h][:, t0:t1, c0:c1])
+            nc.sync.dma_start(out=rows[:, t0:t1, c0:c1], in_=y_view(h, t0, t1, c0, c1))
 
         def store_codes(h, c0, c1):
             flat = out_1[h].rearrange("p n t -> p (n t)")
@@ -161,97 +165,109 @@ def tile_sequence_compressed_values_g6_kernel(
         nc.vector.memset(v_plane[:].bitcast(I32), 0)
         nc.vector.memset(seed[:], 0.0)
         load_c(0, 0)
-        load_scales(nc.scalar, 0)
-        load_scales(nc.scalar, 1)
-        load_scales(nc.gpsimd, 2)
-        load_scales(nc.gpsimd, 3)
+        for q in range(4):
+            load_scales(nc.sync, q)
         nc.scalar.activation(out=warm[:], in_=seed[:, 16:17], func=IDENT)
-        load_v(0, 0)
+        load_v(0, 0, 2)
         nc.sync.dma_start(out=seed[0:P:32, 0:B], in_=seq_factor.partition_broadcast(4))
         for g in range(1, PASSES):
             load_c(0, g)
-            load_v(g, 0)
+            load_v(g, 0, 2 if g == PASSES - 1 else 1)
         nc.sync.dma_start(out=bias[:], in_=slot_bias.rearrange("(h p t) -> p h t", h=HALVES, t=PACK))
         for g in range(PASSES):
             load_v(g, 1)
         for g in range(PASSES):
             load_c(1, g)
 
+        vcopy, scopy = nc.vector.tensor_copy, nc.scalar.copy
         for g in range(PASSES):
-            group_c(0, g, True)
-            if g == 1:
+            if g == 0:
+                group_c(vcopy, 0, g, 0, 1)
+                group_c(scopy, 0, g, 3, 4)
+                group_c(vcopy, 0, g, 1, 2)
+                quant_c(0, g, 0, 1)
+                group_c(vcopy, 0, g, 2, 3)
+                quant_c(0, g, 1, 2)
+                quant_c(0, g, 2, 4)
+            else:
+                group_c(vcopy, 0, g, 0, 2)
+                group_c(scopy, 0, g, 3, 4)
+                group_c(vcopy, 0, g, 2, 3)
+                quant_c(0, g, 0, 2)
+                quant_c(0, g, 2, 4)
+            if g == 0:
                 nc.vector.transpose(out=seed_t[:], in_=seed[:])
-            if g == 2:
+            if g == 1:
                 nc.vector.tensor_copy(out=spread[:], in_=seed_t[:, 0:1].to_broadcast([P, 32]))
-            if g == 3:
+            if g == 2:
                 nc.vector.transpose(out=factor[:], in_=spread[:])
-            quant_c(0, g, 2)
-            if g < PASSES - 1:
+            if g in (1, 2):
                 order = [(b, t) for t in range(PACK) for b in range(2)]
             else:
                 order = [(b, t) for b in range(2) for t in range(PACK)]
             for b, t in order:
                 mm(0, t, b * D, D, g, 4 * b + t)
-        for b in range(2):
-            for t in range(PACK):
-                drain(0, t, b * D, D)
-        for t in (0, 2):
-            store_y(0, t, t + 2, 0, 2 * D)
+        for t in range(PACK):
+            drain(0, t, 0, D)
         group_y(0, 0, D)
         quant_y(0, 0, D)
+        for t in range(PACK):
+            drain(0, t, D, D)
+            if t % 2:
+                store_y(0, t - 1, t + 1, 0, 2 * D)
 
-        group_c(1, 0, False)
+        group_c(vcopy, 1, 0, 0, PACK)
         for g in range(1, PASSES):
-            group_c(1, g, False)
-            quant_c(1, g - 1, 1)
-        quant_c(1, PASSES - 1, 1)
+            group_c(vcopy, 1, g, 0, PACK)
+            quant_c(1, g - 1, 0, PACK)
+        quant_c(1, PASSES - 1, 0, PACK)
 
-        def unit(h, c0, w, bank0, pass_major):
-            if pass_major:
+        def pass_major(h, c0, w, bank0):
+            for g in range(PASSES):
+                for t in range(PACK):
+                    mm(h, t, c0, w, g, bank0 + t)
+            for t in range(PACK):
+                drain(h, t, c0, w)
+
+        def slice_major(h, c0, w, bank0, ts):
+            for t in ts:
                 for g in range(PASSES):
-                    for t in range(PACK):
-                        mm(h, t, c0, w, g, bank0 + t)
-                for t in range(PACK):
-                    drain(h, t, c0, w)
-            else:
-                for t in range(PACK):
-                    for g in range(PASSES):
-                        mm(h, t, c0, w, g, bank0 + t)
-                    drain(h, t, c0, w)
+                    mm(h, t, c0, w, g, bank0 + t)
+                drain(h, t, c0, w)
 
-        unit(0, 2 * D, D, 0, True)
-        unit(0, 3 * D, D, 4, False)
+        pass_major(0, 2 * D, D, 0)
         for t in (0, 2):
+            slice_major(0, 3 * D, D, 4, (t, t + 1))
             store_y(0, t, t + 2, 2 * D, COLS)
         group_y(0, D, D)
-        group_y(0, 2 * D, D)
-        quant_y(0, D, D)
-        group_y(0, 3 * D, D)
-        quant_y(0, 2 * D, D)
-        unit(1, 0, D, 0, True)
-        group_y(1, 0, D)
+        for b in range(2, B):
+            group_y(0, b * D, D)
+            quant_y(0, (b - 1) * D, D)
         quant_y(0, 3 * D, D)
-        quant_y(1, 0, D)
-        unit(1, D, D, 4, False)
+        pass_major(1, 0, D, 0)
+        slice_major(1, D, D, 4, (0, 1))
         store_y(1, 0, 2, 0, 2 * D)
         store_codes(0, 0, COLS)
         for q in range(4):
             store_scales(nc.sync, 0, q)
+        slice_major(1, D, D, 4, (2, 3))
         store_y(1, 2, 4, 0, 2 * D)
+        group_y(1, 0, D)
         group_y(1, D, D)
+        quant_y(1, 0, D)
         quant_y(1, D, D)
         store_codes(1, 0, 2 * D)
-        unit(1, 2 * D, D, 0, False)
+        slice_major(1, 2 * D, D, 0, range(PACK))
         store_y(1, 0, 4, 2 * D, 3 * D)
         group_y(1, 2 * D, D)
         quant_y(1, 2 * D, D)
         half = D // 2
-        unit(1, 3 * D, half, 4, False)
+        slice_major(1, 3 * D, half, 4, range(PACK))
         store_y(1, 0, 4, 3 * D, 3 * D + half)
         group_y(1, 3 * D, half)
         quant_y(1, 3 * D, half)
         store_codes(1, 2 * D, 3 * D + half)
-        unit(1, 3 * D + half, half, 0, False)
+        slice_major(1, 3 * D + half, half, 0, range(PACK))
         store_y(1, 0, 4, 3 * D + half, COLS)
         group_y(1, 3 * D + half, half)
         quant_y(1, 3 * D + half, half)

@@ -30,23 +30,21 @@ def tile_sequence_compressed_values_g6_kernel(
         stage = ctx.enter_context(tc.tile_pool(name="stage", bufs=4))
         psum = ctx.enter_context(tc.psum_pool(name="psum", bufs=1))
         ctx.enter_context(tc.manual_schedule())
+        vcopy, scopy = nc.vector.tensor_copy, nc.scalar.copy
 
-        v_plane = keep.tile([P, COLS], U8, align_bytes=256)
-        seed = keep.tile([P, 32], BF16, align_bytes=64)
-        seed_t = keep.tile([P, 32], BF16, align_bytes=64)
-        spread = keep.tile([P, 32], F32, align_bytes=64)
-        factor = keep.tile([P, 32], F32, align_bytes=64)
-        bias = keep.tile([P, HALVES, PACK], BF16, align_bytes=64)
-        warm = keep.tile([P, 1], F32, align_bytes=64)
+        seed = keep.tile([P, 32], BF16, align_bytes=64, name="seed")
+        seed_t = keep.tile([P, 32], BF16, align_bytes=64, name="seed_t")
+        spread = keep.tile([P, 32], F32, align_bytes=64, name="spread")
+        factor = keep.tile([P, 32], F32, align_bytes=64, name="factor")
+        bias = keep.tile([P, HALVES, PACK], BF16, align_bytes=64, name="bias")
+        zero = keep.tile([P, 32], BF16, align_bytes=64, name="zero")
         v_codes = {}
+        planes = {}
         raw = {}
         c_codes = {}
         c_plane = {}
         for g in range(PASSES):
-            for pair in range(2):
-                v_codes[g, pair] = keep.tile([P, 2 * D], U32, align_bytes=256, name=f"v{g}{pair}")
             for h in range(HALVES):
-                raw[h, g] = keep.tile([P, PACK, GROUP], BF16, align_bytes=256, name=f"raw{h}{g}")
                 c_codes[h, g] = keep.tile([P, GROUP], U32, align_bytes=256, name=f"cc{h}{g}")
                 c_plane[h, g] = keep.tile([P, GROUP], U8, align_bytes=256, name=f"cs{h}{g}")
         y = {}
@@ -54,45 +52,66 @@ def tile_sequence_compressed_values_g6_kernel(
         y_plane = {}
         for h in range(HALVES):
             y_codes[h] = keep.tile([P, COLS], U32, align_bytes=256, name=f"yc{h}")
-            y_plane[h] = keep.tile([P, COLS], U8, align_bytes=256, name=f"ys{h}")
+            y_plane[h] = keep.tile([P, D], U8, align_bytes=256, name=f"ys{h}")
 
-        y_spans = [(0, 0, 2 * D), (0, 2 * D, COLS), (1, 0, 2 * D), (1, 2 * D, 3 * D), (1, 3 * D, 3 * D + D // 2), (1, 3 * D + D // 2, COLS)]
-        for h, c0, c1 in y_spans:
-            y[h, c0, c1] = keep.tile([P, PACK, c1 - c0], F32, align_bytes=256, name=f"y{h}_{c0}")
+        def y_tiles(spans):
+            for h, c0, c1 in spans:
+                y[h, c0, c1] = keep.tile([P, PACK, c1 - c0], F32, align_bytes=256, name=f"y{h}_{c0}")
 
         def y_view(h, t0, t1, c0, c1):
-            for hh, a, b in y_spans:
-                if hh == h and a <= c0 and c1 <= b:
-                    return y[hh, a, b][:, t0:t1, c0 - a : c1 - a]
-            raise ValueError("no such span")
+            key = [k for k in y if k[0] == h and k[1] <= c0 and c1 <= k[2]][0]
+            return y[key][:, t0:t1, c0 - key[1] : c1 - key[1]]
 
-        def load_c(h, g):
-            rows = compress[g * GROUP : (g + 1) * GROUP, h * GROUP : (h + 1) * GROUP]
-            nc.sync.dma_start(out=raw[h, g][:], in_=rows.rearrange("(p j) c -> p j c", j=PACK))
+        def load_c(g, h0, h1):
+            tile = keep.tile([P, PACK, (h1 - h0) * GROUP], BF16, align_bytes=256, name=f"raw{g}{h0}")
+            for h in range(h0, h1):
+                raw[h, g] = tile[:, :, (h - h0) * GROUP : (h - h0 + 1) * GROUP]
+            rows = compress[g * GROUP : (g + 1) * GROUP, h0 * GROUP : h1 * GROUP]
+            nc.sync.dma_start(out=tile[:], in_=rows.rearrange("(p j) c -> p j c", j=PACK))
 
-        def load_v(g, pair, parts=1):
-            flat = v_words[g].rearrange("p n t -> p (n t)")
-            w = 2 * D // parts
-            for i in range(parts):
-                c0 = pair * 2 * D + i * w
-                nc.sync.dma_start(
-                    out=v_codes[g, pair][:, i * w : (i + 1) * w].bitcast(I32),
-                    in_=flat[:, PACK * c0 : PACK * (c0 + w)].bitcast(I32),
+        def load_v(g0, g1, c0, c1):
+            tile = keep.tile([P, g1 - g0, c1 - c0], U32, align_bytes=256, name=f"v{g0}_{c0}")
+            for g in range(g0, g1):
+                for b in range(c0 // D, c1 // D):
+                    v_codes[g, b] = tile[:, g - g0, b * D - c0 : (b + 1) * D - c0]
+            flat = v_words[g0:g1].rearrange("g p n t -> p g (n t)")
+            nc.sync.dma_start(
+                out=tile[:].bitcast(I32),
+                in_=flat[:, :, PACK * c0 : PACK * c1].bitcast(I32),
+            )
+
+        def make_plane(eng, c0, c1):
+            planes[c0, c1] = keep.tile([P, c1 - c0], U8, align_bytes=256, name=f"vs{c0}")
+            eng.memset(planes[c0, c1][:].bitcast(I32), 0)
+
+        def load_scales(eng, c0, c1):
+            for q in range(4):
+                eng.dma_start(
+                    out=planes[c0, c1][32 * q : 32 * q + 16, :].bitcast(I32),
+                    in_=v_scales[:, 4 * q : 4 * q + 4, c0:c1].bitcast(I32),
                 )
 
-        def load_scales(eng, q):
-            eng.dma_start(
-                out=v_plane[32 * q : 32 * q + 16, :].bitcast(I32),
-                in_=v_scales[:, 4 * q : 4 * q + 4, :].bitcast(I32),
-            )
+        def load_seed():
+            nc.sync.dma_start(out=seed[0:P:32, 0:B], in_=seq_factor.partition_broadcast(4))
+
+        def load_bias():
+            nc.sync.dma_start(out=bias[:], in_=slot_bias.rearrange("(h p t) -> p h t", h=HALVES, t=PACK))
+
+        def factor_step(i):
+            if i == 0:
+                nc.vector.transpose(out=seed_t[:], in_=seed[:])
+            if i == 1:
+                nc.vector.tensor_copy(out=spread[:], in_=seed_t[:, 0:1].to_broadcast([P, 32]))
+            if i == 2:
+                nc.vector.transpose(out=factor[:], in_=spread[:])
 
         c_grouped = {}
 
         def group_c(copy, h, g, t0, t1):
-            if t0 == 0:
+            if (h, g) not in c_grouped:
                 c_grouped[h, g] = stage.tile([P, PACK * GROUP], BF16, align_bytes=256, name="c_grouped")
-            dst = c_grouped[h, g][:].rearrange("p (t m j) -> p m t j", t=PACK, j=PACK)
-            src = raw[h, g][:].rearrange("p j (m t) -> p m t j", t=PACK)
+            dst = c_grouped[h, g][:].rearrange("p (t m e j) -> p m t e j", t=PACK, e=2, j=PACK)
+            src = raw[h, g].rearrange("p j (m e t) -> p m t e j", e=2, t=PACK)
             copy(out=dst[:, :, t0:t1], in_=src[:, :, t0:t1])
 
         def quant_c(h, g, t0, t1):
@@ -107,13 +126,13 @@ def tile_sequence_compressed_values_g6_kernel(
         def mm(h, t, c0, w, g, bank):
             if g == 0:
                 acc[h, t, c0] = psum.tile([P, w], F32, name=f"bank{bank}")
-            pair, off = divmod(c0, 2 * D)
+            key = [k for k in planes if k[0] <= c0 < k[1]][0]
             nc.tensor.matmul_mx(
                 out=acc[h, t, c0][:],
                 lhsT=c_codes[h, g][:, t * P : (t + 1) * P].bitcast(FP8X4),
                 lhsT_scale=c_plane[h, g][:, t * P : (t + 1) * P],
-                rhs=v_codes[g, pair][:, off : off + w].bitcast(FP8X4),
-                rhs_scale=v_plane[PACK * g :, c0 : c0 + w],
+                rhs=v_codes[g, c0 // D][:, c0 % D : c0 % D + w].bitcast(FP8X4),
+                rhs_scale=planes[key][PACK * g :, c0 - key[0] : c0 - key[0] + w],
                 start=(g == 0),
                 stop=(g == PASSES - 1),
             )
@@ -130,24 +149,24 @@ def tile_sequence_compressed_values_g6_kernel(
 
         y_grouped = {}
 
-        def group_y(h, c0, w):
-            tile = stage.tile([P, PACK * w], BF16, align_bytes=256, name="y_grouped")
-            y_grouped[h, c0] = tile
-            nc.vector.tensor_copy(
-                out=tile[:].rearrange("p (c i t) -> p c t i", i=4, t=PACK),
-                in_=y_view(h, 0, PACK, c0, c0 + w).rearrange("p t (c i) -> p c t i", i=4),
+        def group_y(h, c0, a=0, b=D, copy=vcopy):
+            if (h, c0) not in y_grouped:
+                y_grouped[h, c0] = stage.tile([P, PACK * D], BF16, align_bytes=256, name="y_grouped")
+            copy(
+                out=y_grouped[h, c0][:, PACK * a : PACK * b].rearrange("p (c i t) -> p c t i", i=4, t=PACK),
+                in_=y_view(h, 0, PACK, c0 + a, c0 + b).rearrange("p t (c i) -> p c t i", i=4),
             )
 
-        def quant_y(h, c0, w):
+        def quant_y(h, c0, a=0, b=D):
             nc.vector.quantize_mx(
-                out=y_codes[h][:, c0 : c0 + w].bitcast(FP8X4),
-                scales=y_plane[h][:, c0 : c0 + w],
-                in_=y_grouped[h, c0][:],
+                out=y_codes[h][:, c0 + a : c0 + b].bitcast(FP8X4),
+                scales=y_plane[h][PACK * (c0 // D) :, a:b],
+                in_=y_grouped[h, c0][:, PACK * a : PACK * b],
             )
 
-        def store_y(h, t0, t1, c0, c1):
+        def store_y(h, t0, t1, c0, c1, eng=nc.sync):
             rows = out_0[h * GROUP : (h + 1) * GROUP].rearrange("(p t) b d -> p t (b d)", t=PACK)
-            nc.sync.dma_start(out=rows[:, t0:t1, c0:c1], in_=y_view(h, t0, t1, c0, c1))
+            eng.dma_start(out=rows[:, t0:t1, c0:c1], in_=y_view(h, t0, t1, c0, c1))
 
         def store_codes(h, c0, c1):
             flat = out_1[h].rearrange("p n t -> p (n t)")
@@ -156,121 +175,155 @@ def tile_sequence_compressed_values_g6_kernel(
                 in_=y_codes[h][:, c0:c1].bitcast(I32),
             )
 
-        def store_scales(eng, h, q):
-            eng.dma_start(
-                out=out_2[h, 4 * q : 4 * q + 4, :].bitcast(I32),
-                in_=y_plane[h][32 * q : 32 * q + 4, :].bitcast(I32),
-            )
+        def store_scales(engs, h):
+            for q in range(4):
+                engs[q % len(engs)].dma_start(
+                    out=out_2[h, 4 * q : 4 * q + 4, :].rearrange("r (b d) -> b r d", b=B).bitcast(I32),
+                    in_=y_plane[h][32 * q : 32 * q + 16, :].bitcast(I32),
+                )
 
-        nc.vector.memset(v_plane[:].bitcast(I32), 0)
-        nc.vector.memset(seed[:], 0.0)
-        load_c(0, 0)
-        for q in range(4):
-            load_scales(nc.sync, q)
-        nc.scalar.activation(out=warm[:], in_=seed[:, 16:17], func=IDENT)
-        load_v(0, 0, 2)
-        nc.sync.dma_start(out=seed[0:P:32, 0:B], in_=seq_factor.partition_broadcast(4))
-        for g in range(1, PASSES):
-            load_c(0, g)
-            load_v(g, 0, 2 if g == PASSES - 1 else 1)
-        nc.sync.dma_start(out=bias[:], in_=slot_bias.rearrange("(h p t) -> p h t", h=HALVES, t=PACK))
-        for g in range(PASSES):
-            load_v(g, 1)
-        for g in range(PASSES):
-            load_c(1, g)
-
-        vcopy, scopy = nc.vector.tensor_copy, nc.scalar.copy
-        for g in range(PASSES):
-            if g == 0:
-                group_c(vcopy, 0, g, 0, 1)
-                group_c(scopy, 0, g, 3, 4)
-                group_c(vcopy, 0, g, 1, 2)
-                quant_c(0, g, 0, 1)
-                group_c(vcopy, 0, g, 2, 3)
-                quant_c(0, g, 1, 2)
-                quant_c(0, g, 2, 4)
-            else:
-                group_c(vcopy, 0, g, 0, 2)
-                group_c(scopy, 0, g, 3, 4)
-                group_c(vcopy, 0, g, 2, 3)
-                quant_c(0, g, 0, 2)
-                quant_c(0, g, 2, 4)
-            if g == 0:
-                nc.vector.transpose(out=seed_t[:], in_=seed[:])
-            if g == 1:
-                nc.vector.tensor_copy(out=spread[:], in_=seed_t[:, 0:1].to_broadcast([P, 32]))
-            if g == 2:
-                nc.vector.transpose(out=factor[:], in_=spread[:])
-            if g in (1, 2):
-                order = [(b, t) for t in range(PACK) for b in range(2)]
-            else:
-                order = [(b, t) for b in range(2) for t in range(PACK)]
-            for b, t in order:
-                mm(0, t, b * D, D, g, 4 * b + t)
-        for t in range(PACK):
-            drain(0, t, 0, D)
-        group_y(0, 0, D)
-        quant_y(0, 0, D)
-        for t in range(PACK):
-            drain(0, t, D, D)
-            if t % 2:
-                store_y(0, t - 1, t + 1, 0, 2 * D)
-
-        group_c(vcopy, 1, 0, 0, PACK)
-        for g in range(1, PASSES):
-            group_c(vcopy, 1, g, 0, PACK)
-            quant_c(1, g - 1, 0, PACK)
-        quant_c(1, PASSES - 1, 0, PACK)
-
-        def pass_major(h, c0, w, bank0):
+        def pass_major(h, c0, bank0, w=D):
             for g in range(PASSES):
                 for t in range(PACK):
                     mm(h, t, c0, w, g, bank0 + t)
             for t in range(PACK):
                 drain(h, t, c0, w)
 
-        def slice_major(h, c0, w, bank0, ts):
+        def slice_major(h, c0, bank0, ts=range(PACK), w=D):
             for t in ts:
                 for g in range(PASSES):
                     mm(h, t, c0, w, g, bank0 + t)
                 drain(h, t, c0, w)
 
-        pass_major(0, 2 * D, D, 0)
-        for t in (0, 2):
-            slice_major(0, 3 * D, D, 4, (t, t + 1))
-            store_y(0, t, t + 2, 2 * D, COLS)
-        group_y(0, D, D)
-        for b in range(2, B):
-            group_y(0, b * D, D)
-            quant_y(0, (b - 1) * D, D)
-        quant_y(0, 3 * D, D)
-        pass_major(1, 0, D, 0)
-        slice_major(1, D, D, 4, (0, 1))
-        store_y(1, 0, 2, 0, 2 * D)
-        store_codes(0, 0, COLS)
-        for q in range(4):
-            store_scales(nc.sync, 0, q)
-        slice_major(1, D, D, 4, (2, 3))
-        store_y(1, 2, 4, 0, 2 * D)
-        group_y(1, 0, D)
-        group_y(1, D, D)
-        quant_y(1, 0, D)
-        quant_y(1, D, D)
+        y_tiles([(0, 0, D), (0, D, 2 * D), (0, 2 * D, COLS), (1, 0, D), (1, D, 2 * D), (1, 2 * D, 3 * D), (1, 3 * D, 3 * D + 256), (1, 3 * D + 256, COLS)])
+        make_plane(nc.vector, 0, 2 * D)
+        nc.vector.memset(zero[:], 0.0)
+        load_c(0, 0, 1)
+        load_scales(nc.sync, 0, 2 * D)
+        nc.scalar.activation(out=seed[:], in_=zero[:], func=IDENT)
+        make_plane(nc.vector, 2 * D, COLS)
+        load_v(0, 1, 0, D)
+        load_v(0, 1, D, 2 * D)
+        load_c(1, 0, 1)
+        load_v(1, 2, 0, 2 * D)
+        load_seed()
+        load_c(2, 0, 1)
+        load_v(2, 3, 0, 2 * D)
+        load_c(3, 0, 1)
+        load_v(3, 4, 0, 2 * D)
+        load_bias()
+        load_v(0, 2, 2 * D, 3 * D)
+        load_scales(nc.sync, 2 * D, COLS)
+        load_v(2, 4, 2 * D, 3 * D)
+        load_c(0, 1, 2)
+        load_v(0, 4, 3 * D, 4 * D)
+        load_c(1, 1, 2)
+        load_c(2, 1, 2)
+        load_c(3, 1, 2)
+        group_c(vcopy, 0, 0, 0, 1)
+        group_c(scopy, 0, 0, 2, 4)
+        group_c(vcopy, 0, 0, 1, 2)
+        quant_c(0, 0, 0, 1)
+        quant_c(0, 0, 1, 2)
+        quant_c(0, 0, 2, 4)
+        for b in range(2):
+            for t in range(PACK):
+                mm(0, t, b * D, D, 0, 4 * b + t)
+        group_c(vcopy, 0, 1, 0, 1)
+        group_c(scopy, 0, 1, 2, 4)
+        group_c(vcopy, 0, 1, 1, 2)
+        quant_c(0, 1, 0, 1)
+        quant_c(0, 1, 1, 2)
+        quant_c(0, 1, 2, 4)
+        factor_step(0)
+        for t in range(PACK):
+            for b in range(2):
+                mm(0, t, b * D, D, 1, 4 * b + t)
+        group_c(vcopy, 0, 2, 0, 1)
+        group_c(scopy, 0, 2, 2, 4)
+        group_c(vcopy, 0, 2, 1, 2)
+        quant_c(0, 2, 0, 1)
+        quant_c(0, 2, 1, 2)
+        quant_c(0, 2, 2, 4)
+        factor_step(1)
+        factor_step(2)
+        for t in range(PACK):
+            for b in range(2):
+                mm(0, t, b * D, D, 2, 4 * b + t)
+        group_c(vcopy, 0, 3, 0, 1)
+        group_c(scopy, 0, 3, 2, 4)
+        group_c(vcopy, 0, 3, 1, 2)
+        quant_c(0, 3, 0, 1)
+        quant_c(0, 3, 1, 2)
+        quant_c(0, 3, 2, 4)
+        for b in range(2):
+            for t in range(PACK):
+                mm(0, t, b * D, D, 3, 4 * b + t)
+        for t in range(PACK):
+            drain(0, t, 0, D)
+        store_y(0, 0, 4, 0, D)
+        group_y(0, 0)
+        for t in range(PACK):
+            drain(0, t, D, D)
+        store_y(0, 0, 4, D, 2 * D)
+        group_c(vcopy, 1, 0, 0, 2)
+        group_c(vcopy, 1, 0, 2, 4)
+        quant_y(0, 0)
+        quant_c(1, 0, 0, 2)
+        quant_c(1, 0, 2, 4)
+        group_y(0, D)
+        group_c(vcopy, 1, 1, 0, 2)
+        group_c(vcopy, 1, 1, 2, 4)
+        quant_y(0, D)
+        quant_c(1, 1, 0, 2)
+        quant_c(1, 1, 2, 4)
+        pass_major(0, 2 * D, 0)
+        slice_major(0, 3 * D, 4, (0, 1))
+        group_c(vcopy, 1, 2, 0, 2)
+        group_c(scopy, 1, 2, 2, 4)
+        slice_major(0, 3 * D, 4, (2, 3))
+        group_c(vcopy, 1, 3, 0, 2)
+        group_c(scopy, 1, 3, 2, 4)
+        quant_c(1, 2, 0, 2)
+        quant_c(1, 2, 2, 4)
+        quant_c(1, 3, 0, 2)
+        quant_c(1, 3, 2, 4)
+        store_y(0, 0, 4, 2 * D, COLS)
+        store_codes(0, 0, 2 * D)
+        group_y(0, 2 * D)
+        group_y(0, 3 * D)
+        quant_y(0, 2 * D)
+        pass_major(1, 0, 0)
+        store_y(1, 0, 4, 0, D)
+        group_y(1, 0, 0, 384)
+        group_y(1, 0, 384, 512, scopy)
+        quant_y(0, 3 * D)
+        store_codes(0, 2 * D, COLS)
+        store_scales([nc.sync], 0)
+        slice_major(1, D, 4)
+        store_y(1, 0, 4, D, 2 * D)
+        quant_y(1, 0)
+        group_y(1, D, 0, 384)
+        group_y(1, D, 384, 512, scopy)
+        quant_y(1, D)
         store_codes(1, 0, 2 * D)
-        slice_major(1, 2 * D, D, 0, range(PACK))
+        slice_major(1, 2 * D, 0)
         store_y(1, 0, 4, 2 * D, 3 * D)
-        group_y(1, 2 * D, D)
-        quant_y(1, 2 * D, D)
-        half = D // 2
-        slice_major(1, 3 * D, half, 4, range(PACK))
-        store_y(1, 0, 4, 3 * D, 3 * D + half)
-        group_y(1, 3 * D, half)
-        quant_y(1, 3 * D, half)
-        store_codes(1, 2 * D, 3 * D + half)
-        slice_major(1, 3 * D + half, half, 0, range(PACK))
-        store_y(1, 0, 4, 3 * D + half, COLS)
-        group_y(1, 3 * D + half, half)
-        quant_y(1, 3 * D + half, half)
-        store_codes(1, 3 * D + half, COLS)
-        for q in range(4):
-            store_scales(nc.scalar if q % 2 else nc.sync, 1, q)
+        group_y(1, 2 * D, 0, 384)
+        group_y(1, 2 * D, 384, 512, scopy)
+        quant_y(1, 2 * D)
+        slice_major(1, 3 * D, 4, w=256)
+        store_y(1, 0, 4, 3 * D, 3 * D + 256)
+        group_y(1, 3 * D, 0, 192)
+        group_y(1, 3 * D, 192, 256, scopy)
+        quant_y(1, 3 * D, 0, 256)
+        store_codes(1, 2 * D, 3 * D + 256)
+        slice_major(1, 3 * D + 256, 0, w=256)
+        store_y(1, 0, 4, 3 * D + 256, COLS)
+        group_y(1, 3 * D, 256, 384)
+        group_y(1, 3 * D, 448, 512, scopy)
+        group_y(1, 3 * D, 384, 448)
+        quant_y(1, 3 * D, 256, 384)
+        quant_y(1, 3 * D, 384, 512)
+        store_codes(1, 3 * D + 256, COLS)
+        store_scales([nc.sync, nc.scalar], 1)

from contextlib import ExitStack

import concourse.mybir as mybir

S, R, B, D = 2048, 1024, 4, 512
FLOPS = 2 * S * R * B * D

F32 = mybir.dt.float32
BF16 = mybir.dt.bfloat16
I32 = mybir.dt.int32
U32 = mybir.dt.uint32
U8 = mybir.dt.uint8
FP8X4 = mybir.dt.float8_e4m3fn_x4
IDENT = mybir.ActivationFunctionType.Identity

P = 128
PACK = 4
GROUP = P * PACK
PASSES = S // GROUP
HALVES = R // GROUP
COLS = B * D


def tile_sequence_compressed_values_g6_kernel(
    tc, v_words, v_scales, compress, seq_factor, slot_bias, out_0, out_1, out_2
):
    nc = tc.nc
    with ExitStack() as ctx:
        keep = ctx.enter_context(tc.tile_pool(name="keep", bufs=1))
        stage = ctx.enter_context(tc.tile_pool(name="stage", bufs=4))
        psum = ctx.enter_context(tc.psum_pool(name="psum", bufs=1))
        ctx.enter_context(tc.manual_schedule())
        vcopy, scopy = nc.vector.tensor_copy, nc.scalar.copy

        seed = keep.tile([P, 32], BF16, align_bytes=64, name="seed")
        seed_t = keep.tile([P, 32], BF16, align_bytes=64, name="seed_t")
        spread = keep.tile([P, 32], F32, align_bytes=64, name="spread")
        factor = keep.tile([P, 32], F32, align_bytes=64, name="factor")
        bias = keep.tile([P, HALVES, PACK], BF16, align_bytes=64, name="bias")
        zero = keep.tile([P, 32], BF16, align_bytes=64, name="zero")
        v_codes = {}
        planes = {}
        raw = {}
        c_codes = {}
        c_plane = {}
        for g in range(PASSES):
            for h in range(HALVES):
                c_codes[h, g] = keep.tile([P, GROUP], U32, align_bytes=256, name=f"cc{h}{g}")
                c_plane[h, g] = keep.tile([P, GROUP], U8, align_bytes=256, name=f"cs{h}{g}")
        y = {}
        y_codes = {}
        y_plane = {}
        for h in range(HALVES):
            y_codes[h] = keep.tile([P, COLS], U32, align_bytes=256, name=f"yc{h}")
            y_plane[h] = keep.tile([P, D], U8, align_bytes=256, name=f"ys{h}")

        def y_tiles(spans):
            for h, c0, c1 in spans:
                y[h, c0, c1] = keep.tile([P, PACK, c1 - c0], F32, align_bytes=256, name=f"y{h}_{c0}")

        def y_view(h, t0, t1, c0, c1):
            key = [k for k in y if k[0] == h and k[1] <= c0 and c1 <= k[2]][0]
            return y[key][:, t0:t1, c0 - key[1] : c1 - key[1]]

        def load_c(g, h0, h1):
            tile = keep.tile([P, PACK, (h1 - h0) * GROUP], BF16, align_bytes=256, name=f"raw{g}{h0}")
            for h in range(h0, h1):
                raw[h, g] = tile[:, :, (h - h0) * GROUP : (h - h0 + 1) * GROUP]
            rows = compress[g * GROUP : (g + 1) * GROUP, h0 * GROUP : h1 * GROUP]
            nc.sync.dma_start(out=tile[:], in_=rows.rearrange("(p j) c -> p j c", j=PACK))

        def load_v(g0, g1, c0, c1):
            tile = keep.tile([P, g1 - g0, c1 - c0], U32, align_bytes=256, name=f"v{g0}_{c0}")
            for g in range(g0, g1):
                for b in range(c0 // D, c1 // D):
                    v_codes[g, b] = tile[:, g - g0, b * D - c0 : (b + 1) * D - c0]
            flat = v_words[g0:g1].rearrange("g p n t -> p g (n t)")
            nc.sync.dma_start(
                out=tile[:].bitcast(I32),
                in_=flat[:, :, PACK * c0 : PACK * c1].bitcast(I32),
            )

        def make_plane(eng, c0, c1):
            planes[c0, c1] = keep.tile([P, c1 - c0], U8, align_bytes=256, name=f"vs{c0}")
            eng.memset(planes[c0, c1][:].bitcast(I32), 0)

        def load_scales(eng, c0, c1):
            for q in range(4):
                eng.dma_start(
                    out=planes[c0, c1][32 * q : 32 * q + 16, :].bitcast(I32),
                    in_=v_scales[:, 4 * q : 4 * q + 4, c0:c1].bitcast(I32),
                )

        def load_seed():
            nc.sync.dma_start(out=seed[0:P:32, 0:B], in_=seq_factor.partition_broadcast(4))

        def load_bias():
            nc.sync.dma_start(out=bias[:], in_=slot_bias.rearrange("(h p t) -> p h t", h=HALVES, t=PACK))

        def factor_step(i):
            if i == 0:
                nc.vector.transpose(out=seed_t[:], in_=seed[:])
            if i == 1:
                nc.vector.tensor_copy(out=spread[:], in_=seed_t[:, 0:1].to_broadcast([P, 32]))
            if i == 2:
                nc.vector.transpose(out=factor[:], in_=spread[:])

        c_grouped = {}

        def group_c(copy, h, g, t0, t1):
            if (h, g) not in c_grouped:
                c_grouped[h, g] = stage.tile([P, PACK * GROUP], BF16, align_bytes=256, name="c_grouped")
            dst = c_grouped[h, g][:].rearrange("p (t m e j) -> p m t e j", t=PACK, e=2, j=PACK)
            src = raw[h, g].rearrange("p j (m e t) -> p m t e j", e=2, t=PACK)
            copy(out=dst[:, :, t0:t1], in_=src[:, :, t0:t1])

        def quant_c(h, g, t0, t1):
            nc.vector.quantize_mx(
                out=c_codes[h, g][:, t0 * P : t1 * P].bitcast(FP8X4),
                scales=c_plane[h, g][:, t0 * P : t1 * P],
                in_=c_grouped[h, g][:, t0 * GROUP : t1 * GROUP],
            )

        acc = {}

        def mm(h, t, c0, w, g, bank):
            if g == 0:
                acc[h, t, c0] = psum.tile([P, w], F32, name=f"bank{bank}")
            key = [k for k in planes if k[0] <= c0 < k[1]][0]
            nc.tensor.matmul_mx(
                out=acc[h, t, c0][:],
                lhsT=c_codes[h, g][:, t * P : (t + 1) * P].bitcast(FP8X4),
                lhsT_scale=c_plane[h, g][:, t * P : (t + 1) * P],
                rhs=v_codes[g, c0 // D][:, c0 % D : c0 % D + w].bitcast(FP8X4),
                rhs_scale=planes[key][PACK * g :, c0 - key[0] : c0 - key[0] + w],
                start=(g == 0),
                stop=(g == PASSES - 1),
            )

        def drain(h, t, c0, w):
            b = c0 // D
            nc.scalar.activation(
                out=y_view(h, t, t + 1, c0, c0 + w)[:, 0],
                in_=acc[h, t, c0][:],
                func=IDENT,
                bias=bias[:, h, t : t + 1],
                scale=factor[:, b : b + 1],
            )

        y_grouped = {}

        def group_y(h, c0, a=0, b=D, copy=vcopy):
            if (h, c0) not in y_grouped:
                y_grouped[h, c0] = stage.tile([P, PACK * D], BF16, align_bytes=256, name="y_grouped")
            copy(
                out=y_grouped[h, c0][:, PACK * a : PACK * b].rearrange("p (c i t) -> p c t i", i=4, t=PACK),
                in_=y_view(h, 0, PACK, c0 + a, c0 + b).rearrange("p t (c i) -> p c t i", i=4),
            )

        def quant_y(h, c0, a=0, b=D):
            nc.vector.quantize_mx(
                out=y_codes[h][:, c0 + a : c0 + b].bitcast(FP8X4),
                scales=y_plane[h][PACK * (c0 // D) :, a:b],
                in_=y_grouped[h, c0][:, PACK * a : PACK * b],
            )

        def store_y(h, t0, t1, c0, c1, eng=nc.sync):
            rows = out_0[h * GROUP : (h + 1) * GROUP].rearrange("(p t) b d -> p t (b d)", t=PACK)
            eng.dma_start(out=rows[:, t0:t1, c0:c1], in_=y_view(h, t0, t1, c0, c1))

        def store_codes(h, c0, c1):
            flat = out_1[h].rearrange("p n t -> p (n t)")
            nc.sync.dma_start(
                out=flat[:, PACK * c0 : PACK * c1].bitcast(I32),
                in_=y_codes[h][:, c0:c1].bitcast(I32),
            )

        def store_scales(engs, h):
            for q in range(4):
                engs[q % len(engs)].dma_start(
                    out=out_2[h, 4 * q : 4 * q + 4, :].rearrange("r (b d) -> b r d", b=B).bitcast(I32),
                    in_=y_plane[h][32 * q : 32 * q + 16, :].bitcast(I32),
                )

        def pass_major(h, c0, bank0, w=D):
            for g in range(PASSES):
                for t in range(PACK):
                    mm(h, t, c0, w, g, bank0 + t)
            for t in range(PACK):
                drain(h, t, c0, w)

        def slice_major(h, c0, bank0, ts=range(PACK), w=D):
            for t in ts:
                for g in range(PASSES):
                    mm(h, t, c0, w, g, bank0 + t)
                drain(h, t, c0, w)

        y_tiles([(0, 0, D), (0, D, 2 * D), (0, 2 * D, COLS), (1, 0, D), (1, D, 2 * D), (1, 2 * D, 3 * D), (1, 3 * D, 3 * D + 256), (1, 3 * D + 256, COLS)])
        make_plane(nc.vector, 0, 2 * D)
        nc.vector.memset(zero[:], 0.0)
        load_c(0, 0, 1)
        load_scales(nc.sync, 0, 2 * D)
        nc.scalar.activation(out=seed[:], in_=zero[:], func=IDENT)
        make_plane(nc.vector, 2 * D, COLS)
        load_v(0, 1, 0, D)
        load_v(0, 1, D, 2 * D)
        load_c(1, 0, 1)
        load_v(1, 2, 0, 2 * D)
        load_seed()
        load_c(2, 0, 1)
        load_v(2, 3, 0, 2 * D)
        load_c(3, 0, 1)
        load_v(3, 4, 0, 2 * D)
        load_bias()
        load_v(0, 2, 2 * D, 3 * D)
        load_scales(nc.sync, 2 * D, COLS)
        load_v(2, 4, 2 * D, 3 * D)
        load_c(0, 1, 2)
        load_v(0, 4, 3 * D, 4 * D)
        load_c(1, 1, 2)
        load_c(2, 1, 2)
        load_c(3, 1, 2)
        group_c(vcopy, 0, 0, 0, 1)
        group_c(scopy, 0, 0, 2, 4)
        group_c(vcopy, 0, 0, 1, 2)
        quant_c(0, 0, 0, 1)
        quant_c(0, 0, 1, 2)
        quant_c(0, 0, 2, 4)
        for b in range(2):
            for t in range(PACK):
                mm(0, t, b * D, D, 0, 4 * b + t)
        group_c(vcopy, 0, 1, 0, 1)
        group_c(scopy, 0, 1, 2, 4)
        group_c(vcopy, 0, 1, 1, 2)
        quant_c(0, 1, 0, 1)
        quant_c(0, 1, 1, 2)
        quant_c(0, 1, 2, 4)
        factor_step(0)
        for t in range(PACK):
            for b in range(2):
                mm(0, t, b * D, D, 1, 4 * b + t)
        group_c(vcopy, 0, 2, 0, 1)
        group_c(scopy, 0, 2, 2, 4)
        group_c(vcopy, 0, 2, 1, 2)
        quant_c(0, 2, 0, 1)
        quant_c(0, 2, 1, 2)
        quant_c(0, 2, 2, 4)
        factor_step(1)
        factor_step(2)
        for t in range(PACK):
            for b in range(2):
                mm(0, t, b * D, D, 2, 4 * b + t)
        group_c(vcopy, 0, 3, 0, 1)
        group_c(scopy, 0, 3, 2, 4)
        group_c(vcopy, 0, 3, 1, 2)
        quant_c(0, 3, 0, 1)
        quant_c(0, 3, 1, 2)
        quant_c(0, 3, 2, 4)
        for b in range(2):
            for t in range(PACK):
                mm(0, t, b * D, D, 3, 4 * b + t)
        for t in range(PACK):
            drain(0, t, 0, D)
        store_y(0, 0, 4, 0, D)
        group_y(0, 0)
        for t in range(PACK):
            drain(0, t, D, D)
        store_y(0, 0, 4, D, 2 * D)
        group_c(vcopy, 1, 0, 0, 2)
        group_c(vcopy, 1, 0, 2, 4)
        quant_y(0, 0)
        quant_c(1, 0, 0, 2)
        quant_c(1, 0, 2, 4)
        group_y(0, D)
        group_c(vcopy, 1, 1, 0, 2)
        group_c(vcopy, 1, 1, 2, 4)
        quant_y(0, D)
        quant_c(1, 1, 0, 2)
        quant_c(1, 1, 2, 4)
        pass_major(0, 2 * D, 0)
        slice_major(0, 3 * D, 4, (0, 1))
        group_c(vcopy, 1, 2, 0, 2)
        group_c(scopy, 1, 2, 2, 4)
        slice_major(0, 3 * D, 4, (2, 3))
        group_c(vcopy, 1, 3, 0, 2)
        group_c(scopy, 1, 3, 2, 4)
        quant_c(1, 2, 0, 2)
        quant_c(1, 2, 2, 4)
        quant_c(1, 3, 0, 2)
        quant_c(1, 3, 2, 4)
        store_y(0, 0, 4, 2 * D, COLS)
        store_codes(0, 0, 2 * D)
        group_y(0, 2 * D)
        group_y(0, 3 * D)
        quant_y(0, 2 * D)
        pass_major(1, 0, 0)
        store_y(1, 0, 4, 0, D)
        group_y(1, 0, 0, 384)
        group_y(1, 0, 384, 512, scopy)
        quant_y(0, 3 * D)
        store_codes(0, 2 * D, COLS)
        store_scales([nc.sync], 0)
        slice_major(1, D, 4)
        store_y(1, 0, 4, D, 2 * D)
        quant_y(1, 0)
        group_y(1, D, 0, 384)
        group_y(1, D, 384, 512, scopy)
        quant_y(1, D)
        store_codes(1, 0, 2 * D)
        slice_major(1, 2 * D, 0)
        store_y(1, 0, 4, 2 * D, 3 * D)
        group_y(1, 2 * D, 0, 384)
        group_y(1, 2 * D, 384, 512, scopy)
        quant_y(1, 2 * D)
        slice_major(1, 3 * D, 4, w=256)
        store_y(1, 0, 4, 3 * D, 3 * D + 256)
        group_y(1, 3 * D, 0, 192)
        group_y(1, 3 * D, 192, 256, scopy)
        quant_y(1, 3 * D, 0, 256)
        store_codes(1, 2 * D, 3 * D + 256)
        slice_major(1, 3 * D + 256, 0, w=256)
        store_y(1, 0, 4, 3 * D + 256, COLS)
        group_y(1, 3 * D, 256, 384)
        group_y(1, 3 * D, 448, 512, scopy)
        group_y(1, 3 * D, 384, 448)
        quant_y(1, 3 * D, 256, 384)
        quant_y(1, 3 * D, 384, 512)
        store_codes(1, 3 * D + 256, COLS)
        store_scales([nc.sync, nc.scalar], 1)
